import numpy as np
import ml_dtypes


def mxq(x, axis, fmt="e4m3"):
    dtype, down = {"e4m3": (ml_dtypes.float8_e4m3fn, 7), "e5m2": (ml_dtypes.float8_e5m2, 14)}[fmt]
    v = np.moveaxis(np.asarray(x, np.float32).astype(ml_dtypes.bfloat16).astype(np.float64), axis, -1)
    blocks = v.reshape(v.shape[:-1] + (-1, 32))
    amax = np.abs(blocks).max(-1, keepdims=True)
    byte = np.maximum(np.where(amax > 0, np.frexp(amax)[1] - 1 + 127, 0) - down, 1)
    scale = np.exp2(byte - 127.0)
    codes = (blocks / scale).astype(np.float32).astype(dtype).astype(np.float64)
    return np.moveaxis((codes * scale).reshape(v.shape), -1, axis)


WIDE = False


def mx_kscale(k):
    if not WIDE:
        return np.ones(k)
    levels = np.array([10, -10, 5, -5, 0])
    if k % 512:
        return np.exp2(np.random.permutation(np.resize(levels, k // 32))).repeat(32)
    a = np.empty((k // 512, 16))
    for p in range(k // 512):
        a[p, :8] = np.random.permutation(np.resize(levels, 8))
        for g in range(8):
            far = levels[np.abs(levels - a[p, g]) >= 10]
            a[p, g + 8] = far[np.random.randint(len(far))]
    return np.exp2(a.ravel()).repeat(32)


def f64(x):
    return np.asarray(x).astype(np.float64)


def striped(idx):
    return np.tile(idx.reshape(-1, 16).T, (8, 1)).astype(np.uint16)


def unstriped(offs):
    return offs[:16].T.reshape(-1).astype(np.int64)


def striped8(idx):
    return np.concatenate([x.reshape(-1, 16).T for x in idx]).astype(np.uint16)


def runs(offs, k):
    lists = np.stack([offs[16 * r : 16 * r + 16].T.reshape(-1) for r in range(8)]).astype(np.int64)
    return lists[np.arange(k) % 512 // 64]


def pack_weight(w):
    k, n = w.shape
    w = f64(np.asarray(w, np.float32).astype(ml_dtypes.bfloat16)).reshape(k // 32, 32, n)
    amax = np.abs(w).max(1)
    byte = np.clip(np.where(amax > 0, np.frexp(amax)[1] - 1 + 127 - 7, 1), 1, 254)
    scaled = (w * np.exp2(127.0 - byte)[:, None, :]).reshape(k, n).astype(np.float32)
    words = np.ascontiguousarray(scaled.reshape(k // 512, 128, 4, n).transpose(0, 1, 3, 2)).astype(ml_dtypes.float8_e4m3fn).view(np.uint8)
    return words, np.ascontiguousarray(byte.astype(np.uint8).reshape(k // 512, 16, n))


def unpack_weight(words, scales):
    g, p, n, _ = words.shape
    vals = np.ascontiguousarray(words).view(ml_dtypes.float8_e4m3fn).astype(np.float64) * np.repeat(np.exp2(scales.astype(np.float64) - 127.0), 8, axis=1)[..., None]
    return vals.transpose(0, 1, 3, 2).reshape(g * 512, n)


K, T, S, V, H = 512, 2048, 512, 512, 512


def setup_inputs():
    n = np.random.standard_normal
    s = mx_kscale(K)[:, None]
    u = mx_kscale(S)
    packed_xT = pack_weight(n((K, T)) * s)
    return {
        "x_words": packed_xT[0],
        "x_scales": packed_xT[1],
        "w1": (n((K, H)) / np.sqrt(K) / s).astype(np.float32),
        "w2": (n((K, H)) / np.sqrt(K) / s).astype(np.float32),
        "ga": (np.random.uniform(0.5, 1.5, (H, 1)) * u[:, None]).astype(np.float32),
        "gb": (np.random.uniform(0.5, 1.5, (H, 1)) / u[:, None]).astype(np.float32),
        "offs": striped(np.random.permutation(T)[:S]),
        "two": striped(np.random.permutation(T)[:V]),
        "n1": striped8(np.stack([np.random.permutation(S) for _ in range(8)])),
        "nq": striped8(np.stack([np.random.permutation(V) for _ in range(8)])),
        "cq": striped8(np.stack([np.random.permutation(V) for _ in range(8)])),
    }


def reference(x_words, x_scales, w1, w2, ga, gb, offs, two, n1, nq, cq):
    xq = unpack_weight(x_words, x_scales)[:, unstriped(offs)]
    a = mxq(f64(w1), 0, "e4m3").T @ xq
    z = f64(ga) * ((a - (a[np.arange(H)[:, None], runs(n1, H)])) ** 2)
    x_two = unpack_weight(x_words, x_scales)[:, unstriped(two)]
    b = mxq(f64(w2), 0, "e4m3").T @ x_two
    z2 = f64(gb) * (np.tanh(b[np.arange(H)[:, None], runs(nq, H)]))
    s = 0.0625 * ((mxq(z, 0, "e4m3").T @ mxq(z2, 0, "e4m3")))
    return np.maximum(s, s[np.arange(S)[:, None], runs(cq, S)])

@@ -1,0 +1,188 @@
+from contextlib import ExitStack
+
+import concourse.mybir as mybir
+
+K, T, S, V, H = 512, 2048, 512, 512, 512
+FLOPS = 3 * 2 * 512 * 512 * 512
+
+F32 = mybir.dt.float32
+BF16 = mybir.dt.bfloat16
+I32 = mybir.dt.int32
+U32 = mybir.dt.uint32
+U16 = mybir.dt.uint16
+U8 = mybir.dt.uint8
+FP8X4 = mybir.dt.float8_e4m3fn_x4
+ALU = mybir.AluOpType
+ACT = mybir.ActivationFunctionType
+
+P = 128
+R = 4
+HALF = 256
+LANES = 16
+V_PIECES = ((0, 256), (256, 128), (384, 128))
+
+
+def entries(lists, start, count):
+    return lists[:, start // LANES : (start + count) // LANES]
+
+
+def tile_picked_keysq_none_p_kernel(tc, x_words, x_scales, w1, w2, ga, gb, offs, two, n1, nq, cq, out):
+    nc = tc.nc
+    with ExitStack() as ctx:
+        lists = ctx.enter_context(tc.tile_pool(name="lists", bufs=1))
+        keep = ctx.enter_context(tc.tile_pool(name="keep", bufs=1))
+        psum = ctx.enter_context(tc.psum_pool(name="psum", bufs=1))
+
+        def sb(name, shape, dtype):
+            return keep.tile(shape, dtype, name=name, tag=name, align_bytes=64)
+
+        def bank(number, width):
+            return psum.tile([P, width], F32, name="bank%d" % number, tag="bank%d" % number)
+
+        offs_sb = lists.tile([P, S // LANES], U16, name="offs_sb")
+        two_sb = lists.tile([P, V // LANES], U16, name="two_sb")
+        n1_sb = lists.tile([P, S // LANES], U16, name="n1_sb")
+        nq_sb = lists.tile([P, V // LANES], U16, name="nq_sb")
+        cq_sb = lists.tile([P, V // LANES], U16, name="cq_sb")
+
+        words = sb("words", [P, T], U32)
+        scales = sb("scales", [P, T], U8)
+        w1_raw = sb("w1_raw", [P, R, H], F32)
+        w2_raw = sb("w2_raw", [P, R, H], F32)
+        ga_sb = sb("ga_sb", [P, R], F32)
+        gb_sb = sb("gb_sb", [P, R], F32)
+
+        nc.sync.dma_start(two_sb[:], two)
+        nc.sync.dma_start(offs_sb[:], offs)
+        for q in range(4):
+            rows = x_scales[0, 4 * q : 4 * q + 4, :].bitcast(I32)
+            nc.sync.dma_start(scales[32 * q : 32 * q + 32, :].bitcast(I32), rows.unsqueeze(0).to_broadcast([8, 4, T // 4]))
+        nc.sync.dma_start(ga_sb[:], ga.rearrange("(p t) o -> p (t o)", t=R))
+        nc.sync.dma_start(w2_raw[:], w2.rearrange("(p j) c -> p j c", j=R))
+        nc.sync.dma_start(gb_sb[:], gb.rearrange("(p t) o -> p (t o)", t=R))
+        nc.sync.dma_start(words[:].bitcast(I32), x_words[0].rearrange("p n r -> p (n r)").bitcast(I32))
+        nc.sync.dma_start(w1_raw[:], w1.rearrange("(p j) c -> p j c", j=R))
+        nc.sync.dma_start(nq_sb[:], nq)
+        nc.sync.dma_start(n1_sb[:], n1)
+        nc.sync.dma_start(cq_sb[:], cq)
+
+        half = sb("half", [P, R], F32)
+        nc.gpsimd.memset(half[:], 0.5)
+        warm = sb("warm", [P, 1], F32)
+        nc.scalar.activation(warm[:], half[:, 0:1], ACT.Tanh)
+
+        nonneg = sb("nonneg", [P, R], F32)
+        sign = sb("sign", [P, R], F32)
+        size = sb("size", [P, R], F32)
+        root = sb("root", [P, R], F32)
+        nc.gpsimd.tensor_scalar(nonneg[:], ga_sb[:], 0.0, 2.0, ALU.is_ge, ALU.mult)
+        nc.gpsimd.tensor_scalar(sign[:], nonneg[:], -1.0, 1.0, ALU.add, ALU.mult)
+        nc.gpsimd.tensor_tensor(size[:], ga_sb[:], sign[:], ALU.mult)
+        nc.gpsimd.tensor_tensor(root[:], size[:], half[:], ALU.pow)
+
+        gb_wide = sb("gb_wide", [P, R, HALF], F32)
+        nc.scalar.copy(gb_wide[:], gb_sb[:].unsqueeze(2).to_broadcast([P, R, HALF]))
+
+        two_scales = sb("two_scales", [P, V], U8)
+        offs_scales = sb("offs_scales", [P, S], U8)
+        two_words = sb("two_words", [P, V], U32)
+        offs_words = sb("offs_words", [P, S], U32)
+        nc.vector.tensor_copy(two_scales[:], scales[:].indirect(two_sb[:]))
+        nc.vector.tensor_copy(offs_scales[:], scales[:].indirect(offs_sb[:]))
+
+        def round_weights(name, raw, pair, copy):
+            rounded = sb("%s_bf%d" % (name, pair), [P, 2, P, R], BF16)
+            copy(rounded[:].rearrange("p t m j -> p m j t"), raw[:].rearrange("p j (m t) -> p m j t", t=R)[:, :, :, 2 * pair : 2 * pair + 2])
+            return rounded
+
+        def quantize(name, values, width):
+            codes = sb(name + "_codes", [P, width], U32)
+            plane = sb(name + "_plane", [P, width], U8)
+            nc.vector.quantize_mx(out=codes[:].bitcast(FP8X4), scales=plane[:], in_=values)
+            return codes, plane
+
+        def product(acc, left, column, right, start, count):
+            nc.tensor.matmul_mx(
+                out=acc,
+                lhsT=left[0][:, column : column + P].bitcast(FP8X4),
+                lhsT_scale=left[1][:, column : column + P],
+                rhs=right[0][:, start : start + count].bitcast(FP8X4),
+                rhs_scale=right[1][:, start : start + count],
+                start=True,
+                stop=True,
+            )
+
+        w2_bf = [round_weights("w2", w2_raw, 0, nc.vector.tensor_copy), round_weights("w2", w2_raw, 1, nc.scalar.copy)]
+        w2_q = [quantize("w2_%d" % pair, w2_bf[pair][:].rearrange("p t m j -> p (t m j)"), 2 * P) for pair in range(2)]
+        for h in range(2):
+            nc.vector.tensor_copy(two_words[:, HALF * h : HALF * (h + 1)], words[:].indirect(entries(two_sb, HALF * h, HALF)))
+        nc.vector.tensor_copy(offs_words[:], words[:].indirect(offs_sb[:]))
+        tanh_b = [sb("tanh_b%d" % t, [P, V], F32) for t in range(R)]
+        for number, (t, start, count) in enumerate(((0, 0, HALF), (0, HALF, HALF), (1, 0, V), (2, 0, V), (3, 0, V))):
+            acc = bank(number, count)
+            product(acc[:], w2_q[t // 2], P * (t % 2), (two_words, two_scales), start, count)
+            nc.scalar.activation(tanh_b[t][:, start : start + count], acc[:], ACT.Tanh, scale=sign[:, t : t + 1])
+
+        def gather_z2(piece, tag):
+            start, count = V_PIECES[piece]
+            planes = keep.tile([P, R, count], F32, name="z2_planes%d" % piece, tag=tag, align_bytes=64)
+            for t in range(R):
+                nc.vector.tensor_tensor(planes[:, t, :], tanh_b[t][:].indirect(entries(nq_sb, start, count)), gb_wide[:, t, 0:count], ALU.mult)
+            return planes
+
+        def round_z2(piece, planes, copy):
+            count = V_PIECES[piece][1]
+            rounded = sb("z2_bf%d" % piece, [P, count, R], BF16)
+            copy(rounded[:].rearrange("p (c i) t -> p c t i", i=4), planes[:].rearrange("p t (c i) -> p c t i", i=4))
+            return rounded
+
+        w1_bf = [round_weights("w1", w1_raw, 0, nc.vector.tensor_copy), round_weights("w1", w1_raw, 1, nc.scalar.copy)]
+        w1_q = [quantize("w1_0", w1_bf[0][:].rearrange("p t m j -> p (t m j)"), 2 * P)]
+        planes0 = gather_z2(0, "z2_planes0")
+        w1_q.append(quantize("w1_1", w1_bf[1][:].rearrange("p t m j -> p (t m j)"), 2 * P))
+
+        diff = [sb("diff%d" % h, [P, R, HALF], F32) for h in range(2)]
+        z_bf = sb("z_bf", [P, R, P, R], BF16)
+        for t in range(R):
+            acc = bank((5 + t) % 8, S)
+            product(acc[:], w1_q[t // 2], P * (t % 2), (offs_words, offs_scales), 0, S)
+            window = sb("a_window%d" % t, [P, S], F32)
+            plain = sb("a_plain%d" % t, [P, S], F32)
+            nc.scalar.activation(window[:], acc[:], ACT.Copy, scale=root[:, t : t + 1])
+            nc.scalar.activation(plain[:], acc[:], ACT.Copy, scale=root[:, t : t + 1])
+            for h in range(2):
+                nc.vector.tensor_tensor(
+                    diff[h][:, t, :], window[:].indirect(entries(n1_sb, HALF * h, HALF)), plain[:, HALF * h : HALF * (h + 1)], ALU.subtract
+                )
+        rounded0 = round_z2(0, planes0, nc.scalar.copy)
+        for h in range(2):
+            nc.scalar.activation(
+                z_bf[:].rearrange("p u m t -> p m t u")[:, 64 * h : 64 * (h + 1)],
+                diff[h][:].rearrange("p t (m u) -> p m t u", u=R),
+                ACT.Square,
+            )
+        planes1 = gather_z2(1, "a_plain3")
+        planes2 = gather_z2(2, "a_window3")
+        rounded1 = round_z2(1, planes1, nc.scalar.copy)
+        rounded2 = round_z2(2, planes2, nc.vector.tensor_copy)
+        z_q = [quantize("z_0", z_bf[:, 0].rearrange("p m t -> p (m t)"), P)]
+        z2_q = [quantize("z2_%d" % i, r[:].rearrange("p v t -> p (v t)"), V_PIECES[i][1]) for i, r in enumerate((rounded0, rounded1, rounded2))]
+        for u in range(1, R):
+            z_q.append(quantize("z_%d" % u, z_bf[:, u].rearrange("p m t -> p (m t)"), P))
+
+        out_rows = out.rearrange("(p u) v -> p u v", u=R)
+        for u in range(R):
+            low, high = bank(2 * u, HALF), bank(2 * u + 1, HALF)
+            product(low[:], z_q[u], 0, z2_q[0], 0, HALF)
+            product(high[:, 0:P], z_q[u], 0, z2_q[1], 0, P)
+            product(high[:, P:HALF], z_q[u], 0, z2_q[2], 0, P)
+            window = sb("s_window%d" % u, [P, V], F32)
+            nc.scalar.activation(window[:, 0:HALF], low[:], ACT.Copy, scale=0.0625)
+            nc.scalar.activation(window[:, HALF:V], high[:], ACT.Copy, scale=0.0625)
+            fetched = [sb("s_fetched%d_%d" % (u, h), [P, HALF], F32) for h in range(2)]
+            for h in range(2):
+                nc.vector.tensor_copy(fetched[h][:], window[:].indirect(entries(cq_sb, HALF * h, HALF)))
+            for h in range(2):
+                larger = sb("s_larger%d_%d" % (u, h), [P, HALF], F32)
+                nc.vector.tensor_tensor(larger[:], fetched[h][:], window[:, HALF * h : HALF * (h + 1)], ALU.max)
+                nc.sync.dma_start(out_rows[:, u, HALF * h : HALF * (h + 1)], larger[:])

@@ -19,7 +19,9 @@ P = 128
 R = 4
 HALF = 256
 LANES = 16
-V_PIECES = ((0, 256), (256, 128), (384, 128))
+EARLY = 384
+LATE = V - EARLY
+POOL_COLUMNS = (V, HALF, 0, 0)
 
 
 def entries(lists, start, count):
@@ -53,13 +55,13 @@ def tile_picked_keysq_none_p_kernel(tc, x_words, x_scales, w1, w2, ga, gb, offs,
         gb_sb = sb("gb_sb", [P, R], F32)
 
         nc.sync.dma_start(two_sb[:], two)
-        nc.sync.dma_start(offs_sb[:], offs)
         for q in range(4):
             rows = x_scales[0, 4 * q : 4 * q + 4, :].bitcast(I32)
             nc.sync.dma_start(scales[32 * q : 32 * q + 32, :].bitcast(I32), rows.unsqueeze(0).to_broadcast([8, 4, T // 4]))
-        nc.sync.dma_start(ga_sb[:], ga.rearrange("(p t) o -> p (t o)", t=R))
-        nc.sync.dma_start(w2_raw[:], w2.rearrange("(p j) c -> p j c", j=R))
+        nc.sync.dma_start(offs_sb[:], offs)
         nc.sync.dma_start(gb_sb[:], gb.rearrange("(p t) o -> p (t o)", t=R))
+        nc.sync.dma_start(w2_raw[:], w2.rearrange("(p j) c -> p j c", j=R))
+        nc.sync.dma_start(ga_sb[:], ga.rearrange("(p t) o -> p (t o)", t=R))
         nc.sync.dma_start(words[:].bitcast(I32), x_words[0].rearrange("p n r -> p (n r)").bitcast(I32))
         nc.sync.dma_start(w1_raw[:], w1.rearrange("(p j) c -> p j c", j=R))
         nc.sync.dma_start(nq_sb[:], nq)
@@ -80,8 +82,8 @@ def tile_picked_keysq_none_p_kernel(tc, x_words, x_scales, w1, w2, ga, gb, offs,
         nc.gpsimd.tensor_tensor(size[:], ga_sb[:], sign[:], ALU.mult)
         nc.gpsimd.tensor_tensor(root[:], size[:], half[:], ALU.pow)
 
-        gb_wide = sb("gb_wide", [P, R, HALF], F32)
-        nc.scalar.copy(gb_wide[:], gb_sb[:].unsqueeze(2).to_broadcast([P, R, HALF]))
+        gb_wide = sb("gb_wide", [P, R, EARLY], F32)
+        nc.scalar.copy(gb_wide[:], gb_sb[:].unsqueeze(2).to_broadcast([P, R, EARLY]))
 
         two_scales = sb("two_scales", [P, V], U8)
         offs_scales = sb("offs_scales", [P, S], U8)
@@ -90,16 +92,16 @@ def tile_picked_keysq_none_p_kernel(tc, x_words, x_scales, w1, w2, ga, gb, offs,
         nc.vector.tensor_copy(two_scales[:], scales[:].indirect(two_sb[:]))
         nc.vector.tensor_copy(offs_scales[:], scales[:].indirect(offs_sb[:]))
 
-        def round_weights(name, raw, pair, copy):
-            rounded = sb("%s_bf%d" % (name, pair), [P, 2, P, R], BF16)
-            copy(rounded[:].rearrange("p t m j -> p m j t"), raw[:].rearrange("p j (m t) -> p m j t", t=R)[:, :, :, 2 * pair : 2 * pair + 2])
-            return rounded
-
         def quantize(name, values, width):
             codes = sb(name + "_codes", [P, width], U32)
             plane = sb(name + "_plane", [P, width], U8)
             nc.vector.quantize_mx(out=codes[:].bitcast(FP8X4), scales=plane[:], in_=values)
             return codes, plane
+
+        def quantize_weights(name, raw, pair, copy):
+            rounded = sb("%s_bf%d" % (name, pair), [P, 2, P, R], BF16)
+            copy(rounded[:].rearrange("p t m j -> p m j t"), raw[:].rearrange("p j (m t) -> p m j t", t=R)[:, :, :, 2 * pair : 2 * pair + 2])
+            return quantize("%s_%d" % (name, pair), rounded[:].rearrange("p t m j -> p (t m j)"), 2 * P)
 
         def product(acc, left, column, right, start, count):
             nc.tensor.matmul_mx(
@@ -112,38 +114,33 @@ def tile_picked_keysq_none_p_kernel(tc, x_words, x_scales, w1, w2, ga, gb, offs,
                 stop=True,
             )
 
-        w2_bf = [round_weights("w2", w2_raw, 0, nc.vector.tensor_copy), round_weights("w2", w2_raw, 1, nc.scalar.copy)]
-        w2_q = [quantize("w2_%d" % pair, w2_bf[pair][:].rearrange("p t m j -> p (t m j)"), 2 * P) for pair in range(2)]
+        w2_q = [quantize_weights("w2", w2_raw, 0, nc.vector.tensor_copy), quantize_weights("w2", w2_raw, 1, nc.scalar.copy)]
         for h in range(2):
             nc.vector.tensor_copy(two_words[:, HALF * h : HALF * (h + 1)], words[:].indirect(entries(two_sb, HALF * h, HALF)))
         nc.vector.tensor_copy(offs_words[:], words[:].indirect(offs_sb[:]))
         tanh_b = [sb("tanh_b%d" % t, [P, V], F32) for t in range(R)]
-        for number, (t, start, count) in enumerate(((0, 0, HALF), (0, HALF, HALF), (1, 0, V), (2, 0, V), (3, 0, V))):
+
+
+        def make_tanh(number, t, start, count):
             acc = bank(number, count)
             product(acc[:], w2_q[t // 2], P * (t % 2), (two_words, two_scales), start, count)
             nc.scalar.activation(tanh_b[t][:, start : start + count], acc[:], ACT.Tanh, scale=sign[:, t : t + 1])
 
-        def gather_z2(piece, tag):
-            start, count = V_PIECES[piece]
-            planes = keep.tile([P, R, count], F32, name="z2_planes%d" % piece, tag=tag, align_bytes=64)
-            for t in range(R):
-                nc.vector.tensor_tensor(planes[:, t, :], tanh_b[t][:].indirect(entries(nq_sb, start, count)), gb_wide[:, t, 0:count], ALU.mult)
-            return planes
+        def gather_early(t):
+            nc.vector.tensor_tensor(early[:, t, :], tanh_b[t][:].indirect(entries(nq_sb, 0, EARLY)), gb_wide[:, t, :], ALU.mult)
 
-        def round_z2(piece, planes, copy):
-            count = V_PIECES[piece][1]
-            rounded = sb("z2_bf%d" % piece, [P, count, R], BF16)
-            copy(rounded[:].rearrange("p (c i) t -> p c t i", i=4), planes[:].rearrange("p t (c i) -> p c t i", i=4))
-            return rounded
-
-        w1_bf = [round_weights("w1", w1_raw, 0, nc.vector.tensor_copy), round_weights("w1", w1_raw, 1, nc.scalar.copy)]
-        w1_q = [quantize("w1_0", w1_bf[0][:].rearrange("p t m j -> p (t m j)"), 2 * P)]
-        planes0 = gather_z2(0, "z2_planes0")
-        w1_q.append(quantize("w1_1", w1_bf[1][:].rearrange("p t m j -> p (t m j)"), 2 * P))
+        make_tanh(0, 0, 0, HALF)
+        make_tanh(1, 0, HALF, HALF)
+        for t in range(1, R):
+            make_tanh(t + 1, t, 0, V)
+        w1_q = [quantize_weights("w1", w1_raw, 0, nc.vector.tensor_copy), quantize_weights("w1", w1_raw, 1, nc.scalar.copy)]
+        early = keep.tile([P, R, EARLY], F32, name="z2_early", tag="w1_bf0", align_bytes=64)
+        for t in range(R):
+            gather_early(t)
 
         diff = [sb("diff%d" % h, [P, R, HALF], F32) for h in range(2)]
-        z_bf = sb("z_bf", [P, R, P, R], BF16)
-        for t in range(R):
+
+        def make_diff(t):
             acc = bank((5 + t) % 8, S)
             product(acc[:], w1_q[t // 2], P * (t % 2), (offs_words, offs_scales), 0, S)
             window = sb("a_window%d" % t, [P, S], F32)
@@ -154,35 +151,54 @@ def tile_picked_keysq_none_p_kernel(tc, x_words, x_scales, w1, w2, ga, gb, offs,
                 nc.vector.tensor_tensor(
                     diff[h][:, t, :], window[:].indirect(entries(n1_sb, HALF * h, HALF)), plain[:, HALF * h : HALF * (h + 1)], ALU.subtract
                 )
-        rounded0 = round_z2(0, planes0, nc.scalar.copy)
+
+        for t in range(R):
+            make_diff(t)
+        early_bf = keep.tile([P, EARLY, R], BF16, name="z2_early_bf", tag="w1_1_codes", align_bytes=64)
+        nc.scalar.copy(early_bf[:].rearrange("p (c i) t -> p c t i", i=4), early[:].rearrange("p t (c i) -> p c t i", i=4))
+        z_bf = sb("z_bf", [P, R, P, R], BF16)
         for h in range(2):
             nc.scalar.activation(
                 z_bf[:].rearrange("p u m t -> p m t u")[:, 64 * h : 64 * (h + 1)],
                 diff[h][:].rearrange("p t (m u) -> p m t u", u=R),
                 ACT.Square,
             )
-        planes1 = gather_z2(1, "a_plain3")
-        planes2 = gather_z2(2, "a_window3")
-        rounded1 = round_z2(1, planes1, nc.scalar.copy)
-        rounded2 = round_z2(2, planes2, nc.vector.tensor_copy)
-        z_q = [quantize("z_0", z_bf[:, 0].rearrange("p m t -> p (m t)"), P)]
-        z2_q = [quantize("z2_%d" % i, r[:].rearrange("p v t -> p (v t)"), V_PIECES[i][1]) for i, r in enumerate((rounded0, rounded1, rounded2))]
-        for u in range(1, R):
-            z_q.append(quantize("z_%d" % u, z_bf[:, u].rearrange("p m t -> p (m t)"), P))
+
+        late = keep.tile([P, R, LATE], F32, name="z2_late", tag="a_window3", align_bytes=64)
+        for t in range(R):
+            nc.vector.tensor_tensor(late[:, t, :], tanh_b[t][:].indirect(entries(nq_sb, EARLY, LATE)), gb_wide[:, t, 0:LATE], ALU.mult)
+        late_bf = sb("z2_late_bf", [P, LATE, R], BF16)
+        nc.vector.tensor_copy(late_bf[:].rearrange("p (c i) t -> p c t i", i=4), late[:].rearrange("p t (c i) -> p c t i", i=4))
+        z2_codes = sb("z2_codes", [P, V], U32)
+        z2_plane = sb("z2_plane", [P, V], U8)
+        for start, count, values in ((0, HALF, early_bf[:, 0:HALF]), (HALF, EARLY - HALF, early_bf[:, HALF:EARLY]), (EARLY, LATE, late_bf[:])):
+            nc.vector.quantize_mx(
+                out=z2_codes[:, start : start + count].bitcast(FP8X4),
+                scales=z2_plane[:, start : start + count],
+                in_=values.rearrange("p v t -> p (v t)"),
+            )
+        z_q = [quantize("z_%d" % u, z_bf[:, u].rearrange("p m t -> p (m t)"), P) for u in range(R)]
 
         out_rows = out.rearrange("(p u) v -> p u v", u=R)
         for u in range(R):
-            low, high = bank(2 * u, HALF), bank(2 * u + 1, HALF)
-            product(low[:], z_q[u], 0, z2_q[0], 0, HALF)
-            product(high[:, 0:P], z_q[u], 0, z2_q[1], 0, P)
-            product(high[:, P:HALF], z_q[u], 0, z2_q[2], 0, P)
             window = sb("s_window%d" % u, [P, V], F32)
-            nc.scalar.activation(window[:, 0:HALF], low[:], ACT.Copy, scale=0.0625)
-            nc.scalar.activation(window[:, HALF:V], high[:], ACT.Copy, scale=0.0625)
-            fetched = [sb("s_fetched%d_%d" % (u, h), [P, HALF], F32) for h in range(2)]
+            accs = [bank(2 * u + h, HALF) for h in range(2)]
             for h in range(2):
-                nc.vector.tensor_copy(fetched[h][:], window[:].indirect(entries(cq_sb, HALF * h, HALF)))
+                product(accs[h][:], z_q[u], 0, (z2_codes, z2_plane), HALF * h, HALF)
+                nc.scalar.activation(window[:, HALF * h : HALF * (h + 1)], accs[h][:], ACT.Copy, scale=0.0625)
+            fetched = sb("s_fetched%d" % u, [P, V], F32)
+            larger = sb("s_larger%d" % u, [P, V], F32)
             for h in range(2):
-                larger = sb("s_larger%d_%d" % (u, h), [P, HALF], F32)
-                nc.vector.tensor_tensor(larger[:], fetched[h][:], window[:, HALF * h : HALF * (h + 1)], ALU.max)
-                nc.sync.dma_start(out_rows[:, u, HALF * h : HALF * (h + 1)], larger[:])
+                nc.vector.tensor_copy(fetched[:, HALF * h : HALF * (h + 1)], window[:].indirect(entries(cq_sb, HALF * h, HALF)))
+            count = POOL_COLUMNS[u]
+            if count:
+                excess = sb("s_excess%d" % u, [P, count], F32)
+                gain = sb("s_gain%d" % u, [P, count], F32)
+                nc.gpsimd.tensor_tensor(excess[:], fetched[:, 0:count], window[:, 0:count], ALU.subtract)
+                nc.scalar.activation(gain[:], excess[:], ACT.Relu)
+                nc.gpsimd.tensor_tensor(larger[:, 0:count], gain[:], window[:, 0:count], ALU.add)
+                nc.scalar.dma_start(out_rows[:, u, 0:count], larger[:, 0:count])
+            for h in range(count // HALF, 2):
+                columns = slice(HALF * h, HALF * (h + 1))
+                nc.vector.scalar_tensor_tensor(larger[:, columns], accs[h][:], 0.0625, fetched[:, columns], ALU.mult, ALU.max)
+                nc.sync.dma_start(out_rows[:, u, columns], larger[:, columns])

@@ -59,12 +59,12 @@ def tile_picked_keysq_none_p_kernel(tc, x_words, x_scales, w1, w2, ga, gb, offs,
             rows = x_scales[0, 4 * q : 4 * q + 4, :].bitcast(I32)
             nc.sync.dma_start(scales[32 * q : 32 * q + 32, :].bitcast(I32), rows.unsqueeze(0).to_broadcast([8, 4, T // 4]))
         nc.sync.dma_start(offs_sb[:], offs)
-        nc.sync.dma_start(gb_sb[:], gb.rearrange("(p t) o -> p (t o)", t=R))
-        nc.sync.dma_start(w2_raw[:], w2.rearrange("(p j) c -> p j c", j=R))
         nc.sync.dma_start(ga_sb[:], ga.rearrange("(p t) o -> p (t o)", t=R))
         nc.sync.dma_start(words[:].bitcast(I32), x_words[0].rearrange("p n r -> p (n r)").bitcast(I32))
-        nc.sync.dma_start(w1_raw[:], w1.rearrange("(p j) c -> p j c", j=R))
+        nc.sync.dma_start(gb_sb[:], gb.rearrange("(p t) o -> p (t o)", t=R))
+        nc.sync.dma_start(w2_raw[:], w2.rearrange("(p j) c -> p j c", j=R))
         nc.sync.dma_start(nq_sb[:], nq)
+        nc.sync.dma_start(w1_raw[:], w1.rearrange("(p j) c -> p j c", j=R))
         nc.sync.dma_start(n1_sb[:], n1)
         nc.sync.dma_start(cq_sb[:], cq)
 
@@ -91,6 +91,8 @@ def tile_picked_keysq_none_p_kernel(tc, x_words, x_scales, w1, w2, ga, gb, offs,
         offs_words = sb("offs_words", [P, S], U32)
         nc.vector.tensor_copy(two_scales[:], scales[:].indirect(two_sb[:]))
         nc.vector.tensor_copy(offs_scales[:], scales[:].indirect(offs_sb[:]))
+        nc.vector.tensor_copy(two_words[:], words[:].indirect(two_sb[:]))
+        nc.vector.tensor_copy(offs_words[:], words[:].indirect(offs_sb[:]))
 
         def quantize(name, values, width):
             codes = sb(name + "_codes", [P, width], U32)
@@ -115,9 +117,6 @@ def tile_picked_keysq_none_p_kernel(tc, x_words, x_scales, w1, w2, ga, gb, offs,
             )
 
         w2_q = [quantize_weights("w2", w2_raw, 0, nc.vector.tensor_copy), quantize_weights("w2", w2_raw, 1, nc.scalar.copy)]
-        for h in range(2):
-            nc.vector.tensor_copy(two_words[:, HALF * h : HALF * (h + 1)], words[:].indirect(entries(two_sb, HALF * h, HALF)))
-        nc.vector.tensor_copy(offs_words[:], words[:].indirect(offs_sb[:]))
         tanh_b = [sb("tanh_b%d" % t, [P, V], F32) for t in range(R)]
 
 
@@ -167,25 +166,39 @@ def tile_picked_keysq_none_p_kernel(tc, x_words, x_scales, w1, w2, ga, gb, offs,
         late = keep.tile([P, R, LATE], F32, name="z2_late", tag="a_window3", align_bytes=64)
         for t in range(R):
             nc.vector.tensor_tensor(late[:, t, :], tanh_b[t][:].indirect(entries(nq_sb, EARLY, LATE)), gb_wide[:, t, 0:LATE], ALU.mult)
-        late_bf = sb("z2_late_bf", [P, LATE, R], BF16)
-        nc.vector.tensor_copy(late_bf[:].rearrange("p (c i) t -> p c t i", i=4), late[:].rearrange("p t (c i) -> p c t i", i=4))
         z2_codes = sb("z2_codes", [P, V], U32)
         z2_plane = sb("z2_plane", [P, V], U8)
-        for start, count, values in ((0, HALF, early_bf[:, 0:HALF]), (HALF, EARLY - HALF, early_bf[:, HALF:EARLY]), (EARLY, LATE, late_bf[:])):
+
+        def quantize_z2(start, count, values):
             nc.vector.quantize_mx(
                 out=z2_codes[:, start : start + count].bitcast(FP8X4),
                 scales=z2_plane[:, start : start + count],
                 in_=values.rearrange("p v t -> p (v t)"),
             )
-        z_q = [quantize("z_%d" % u, z_bf[:, u].rearrange("p m t -> p (m t)"), P) for u in range(R)]
 
+        def quantize_z(u):
+            return quantize("z_%d" % u, z_bf[:, u].rearrange("p m t -> p (m t)"), P)
+
+        quantize_z2(0, HALF, early_bf[:, 0:HALF])
+        quantize_z2(HALF, EARLY - HALF, early_bf[:, HALF:EARLY])
+        z_q = [quantize_z(0)]
+        late_bf = z_bf[:, 0]
+        nc.vector.tensor_copy(late_bf.rearrange("p (c i) t -> p c t i", i=4), late[:].rearrange("p t (c i) -> p c t i", i=4))
+        quantize_z2(EARLY, LATE, late_bf)
+        z_q.extend(quantize_z(u) for u in range(1, R))
+
+        next_bank = 0
         out_rows = out.rearrange("(p u) v -> p u v", u=R)
         for u in range(R):
             window = sb("s_window%d" % u, [P, V], F32)
-            accs = [bank(2 * u + h, HALF) for h in range(2)]
-            for h in range(2):
-                product(accs[h][:], z_q[u], 0, (z2_codes, z2_plane), HALF * h, HALF)
-                nc.scalar.activation(window[:, HALF * h : HALF * (h + 1)], accs[h][:], ACT.Copy, scale=0.0625)
+            pieces = ((0, HALF), (HALF, EARLY - HALF), (EARLY, LATE)) if u == 0 else ((0, HALF), (HALF, HALF))
+            accs = []
+            for start, count in pieces:
+                acc = bank(next_bank % 8, count)
+                next_bank += 1
+                product(acc[:], z_q[u], 0, (z2_codes, z2_plane), start, count)
+                nc.scalar.activation(window[:, start : start + count], acc[:], ACT.Copy, scale=0.0625)
+                accs.append(acc)
             fetched = sb("s_fetched%d" % u, [P, V], F32)
             larger = sb("s_larger%d" % u, [P, V], F32)
             for h in range(2):

@@ -21,7 +21,7 @@ HALF = 256
 LANES = 16
 EARLY = 384
 LATE = V - EARLY
-POOL_COLUMNS = (V, HALF, 0, 0)
+POOL_COLUMNS = (V, 384, 0, 0)
 
 
 def entries(lists, start, count):
@@ -49,7 +49,7 @@ def tile_picked_keysq_none_p_kernel(tc, x_words, x_scales, w1, w2, ga, gb, offs,
 
         words = sb("words", [P, T], U32)
         scales = sb("scales", [P, T], U8)
-        w1_raw = sb("w1_raw", [P, R, H], F32)
+        w1_raw = [sb("w1_raw%d" % h, [P, R, HALF], F32) for h in range(2)]
         w2_raw = sb("w2_raw", [P, R, H], F32)
         ga_sb = sb("ga_sb", [P, R], F32)
         gb_sb = sb("gb_sb", [P, R], F32)
@@ -63,8 +63,9 @@ def tile_picked_keysq_none_p_kernel(tc, x_words, x_scales, w1, w2, ga, gb, offs,
         nc.sync.dma_start(words[:].bitcast(I32), x_words[0].rearrange("p n r -> p (n r)").bitcast(I32))
         nc.sync.dma_start(gb_sb[:], gb.rearrange("(p t) o -> p (t o)", t=R))
         nc.sync.dma_start(w2_raw[:], w2.rearrange("(p j) c -> p j c", j=R))
+        for h in range(2):
+            nc.sync.dma_start(w1_raw[h][:], w1.rearrange("(p j) c -> p j c", j=R)[:, :, HALF * h : HALF * (h + 1)])
         nc.sync.dma_start(nq_sb[:], nq)
-        nc.sync.dma_start(w1_raw[:], w1.rearrange("(p j) c -> p j c", j=R))
         nc.sync.dma_start(n1_sb[:], n1)
         nc.sync.dma_start(cq_sb[:], cq)
 
@@ -100,10 +101,11 @@ def tile_picked_keysq_none_p_kernel(tc, x_words, x_scales, w1, w2, ga, gb, offs,
             nc.vector.quantize_mx(out=codes[:].bitcast(FP8X4), scales=plane[:], in_=values)
             return codes, plane
 
-        def quantize_weights(name, raw, pair, copy):
-            rounded = sb("%s_bf%d" % (name, pair), [P, 2, P, R], BF16)
-            copy(rounded[:].rearrange("p t m j -> p m j t"), raw[:].rearrange("p j (m t) -> p m j t", t=R)[:, :, :, 2 * pair : 2 * pair + 2])
-            return quantize("%s_%d" % (name, pair), rounded[:].rearrange("p t m j -> p (t m j)"), 2 * P)
+        def round_weights(rounded, raw, pair, copy):
+            copy(rounded.rearrange("p t m j -> p m j t"), raw.rearrange("p j (m t) -> p m j t", t=R)[:, :, :, 2 * pair : 2 * pair + 2])
+
+        def quantize_pair(name, rounded):
+            return quantize(name, rounded[:].rearrange("p t m j -> p (t m j)"), 2 * P)
 
         def product(acc, left, column, right, start, count):
             nc.tensor.matmul_mx(
@@ -116,7 +118,10 @@ def tile_picked_keysq_none_p_kernel(tc, x_words, x_scales, w1, w2, ga, gb, offs,
                 stop=True,
             )
 
-        w2_q = [quantize_weights("w2", w2_raw, 0, nc.vector.tensor_copy), quantize_weights("w2", w2_raw, 1, nc.scalar.copy)]
+        w2_bf = [sb("w2_bf%d" % pair, [P, 2, P, R], BF16) for pair in range(2)]
+        round_weights(w2_bf[0][:], w2_raw[:], 0, nc.vector.tensor_copy)
+        round_weights(w2_bf[1][:], w2_raw[:], 1, nc.scalar.copy)
+        w2_q = [quantize_pair("w2_%d" % pair, w2_bf[pair]) for pair in range(2)]
         tanh_b = [sb("tanh_b%d" % t, [P, V], F32) for t in range(R)]
 
 
@@ -132,20 +137,26 @@ def tile_picked_keysq_none_p_kernel(tc, x_words, x_scales, w1, w2, ga, gb, offs,
         make_tanh(1, 0, HALF, HALF)
         for t in range(1, R):
             make_tanh(t + 1, t, 0, V)
-        w1_q = [quantize_weights("w1", w1_raw, 0, nc.vector.tensor_copy), quantize_weights("w1", w1_raw, 1, nc.scalar.copy)]
+        w1_bf = [sb("w1_bf%d" % pair, [P, 2, P, R], BF16) for pair in range(2)]
+        round_weights(w1_bf[0][:, :, 0:64], w1_raw[0][:], 0, nc.vector.tensor_copy)
+        round_weights(w1_bf[1][:, :, 0:64], w1_raw[0][:], 1, nc.vector.tensor_copy)
+        round_weights(w1_bf[0][:, :, 64:P], w1_raw[1][:], 0, nc.vector.tensor_copy)
+        round_weights(w1_bf[1][:, :, 64:P], w1_raw[1][:], 1, nc.scalar.copy)
+        w1_q = [quantize_pair("w1_%d" % pair, w1_bf[pair]) for pair in range(2)]
         early = keep.tile([P, R, EARLY], F32, name="z2_early", tag="w1_bf0", align_bytes=64)
         for t in range(R):
             gather_early(t)
 
+        s_tiles = [sb("s_tile%d" % u, [P, 2 * V], F32) for u in range(R)]
         diff = [sb("diff%d" % h, [P, R, HALF], F32) for h in range(2)]
 
         def make_diff(t):
             acc = bank((5 + t) % 8, S)
             product(acc[:], w1_q[t // 2], P * (t % 2), (offs_words, offs_scales), 0, S)
             window = sb("a_window%d" % t, [P, S], F32)
-            plain = sb("a_plain%d" % t, [P, S], F32)
+            plain = s_tiles[t][:, V : 2 * V]
             nc.scalar.activation(window[:], acc[:], ACT.Copy, scale=root[:, t : t + 1])
-            nc.scalar.activation(plain[:], acc[:], ACT.Copy, scale=root[:, t : t + 1])
+            nc.scalar.activation(plain, acc[:], ACT.Copy, scale=root[:, t : t + 1])
             for h in range(2):
                 nc.vector.tensor_tensor(
                     diff[h][:, t, :], window[:].indirect(entries(n1_sb, HALF * h, HALF)), plain[:, HALF * h : HALF * (h + 1)], ALU.subtract
@@ -190,28 +201,29 @@ def tile_picked_keysq_none_p_kernel(tc, x_words, x_scales, w1, w2, ga, gb, offs,
         next_bank = 0
         out_rows = out.rearrange("(p u) v -> p u v", u=R)
         for u in range(R):
-            window = sb("s_window%d" % u, [P, V], F32)
-            pieces = ((0, HALF), (HALF, EARLY - HALF), (EARLY, LATE)) if u == 0 else ((0, HALF), (HALF, HALF))
-            accs = []
+            window = s_tiles[u]
+            pieces = ((0, HALF), (HALF, EARLY - HALF), (EARLY, LATE)) if u == 0 else ((0, V),)
             for start, count in pieces:
-                acc = bank(next_bank % 8, count)
+                acc = bank(next_bank, count)
                 next_bank += 1
                 product(acc[:], z_q[u], 0, (z2_codes, z2_plane), start, count)
                 nc.scalar.activation(window[:, start : start + count], acc[:], ACT.Copy, scale=0.0625)
-                accs.append(acc)
             fetched = sb("s_fetched%d" % u, [P, V], F32)
             larger = sb("s_larger%d" % u, [P, V], F32)
-            for h in range(2):
-                nc.vector.tensor_copy(fetched[:, HALF * h : HALF * (h + 1)], window[:].indirect(entries(cq_sb, HALF * h, HALF)))
-            count = POOL_COLUMNS[u]
-            if count:
-                excess = sb("s_excess%d" % u, [P, count], F32)
-                gain = sb("s_gain%d" % u, [P, count], F32)
-                nc.gpsimd.tensor_tensor(excess[:], fetched[:, 0:count], window[:, 0:count], ALU.subtract)
+            split = POOL_COLUMNS[u]
+            if split:
+                excess = sb("s_excess%d" % u, [P, split], F32)
+                gain = sb("s_gain%d" % u, [P, split], F32)
+                nc.vector.tensor_copy(fetched[:], window[:].indirect(cq_sb[:]))
+                nc.gpsimd.tensor_tensor(excess[:], fetched[:, 0:split], window[:, 0:split], ALU.subtract)
                 nc.scalar.activation(gain[:], excess[:], ACT.Relu)
-                nc.gpsimd.tensor_tensor(larger[:, 0:count], gain[:], window[:, 0:count], ALU.add)
-                nc.scalar.dma_start(out_rows[:, u, 0:count], larger[:, 0:count])
-            for h in range(count // HALF, 2):
-                columns = slice(HALF * h, HALF * (h + 1))
-                nc.vector.scalar_tensor_tensor(larger[:, columns], accs[h][:], 0.0625, fetched[:, columns], ALU.mult, ALU.max)
+                nc.gpsimd.tensor_tensor(larger[:, 0:split], gain[:], window[:, 0:split], ALU.add)
+                nc.scalar.dma_start(out_rows[:, u, 0:split], larger[:, 0:split])
+                rest = [slice(split, V)] if split < V else []
+            else:
+                rest = [slice(0, HALF), slice(HALF, V)]
+                for columns in rest:
+                    nc.vector.tensor_copy(fetched[:, columns], window[:].indirect(entries(cq_sb, columns.start, HALF)))
+            for columns in rest:
+                nc.vector.scalar_tensor_tensor(larger[:, columns], acc[:, columns], 0.0625, fetched[:, columns], ALU.mult, ALU.max)
                 nc.sync.dma_start(out_rows[:, u, columns], larger[:, columns])

from contextlib import ExitStack

import concourse.mybir as mybir

K, T, S, V, H = 512, 2048, 512, 512, 512
FLOPS = 3 * 2 * 512 * 512 * 512

F32 = mybir.dt.float32
BF16 = mybir.dt.bfloat16
I32 = mybir.dt.int32
U32 = mybir.dt.uint32
U16 = mybir.dt.uint16
U8 = mybir.dt.uint8
FP8X4 = mybir.dt.float8_e4m3fn_x4
ALU = mybir.AluOpType
ACT = mybir.ActivationFunctionType

P = 128
R = 4
HALF = 256
LANES = 16
EARLY = 384
LATE = V - EARLY
POOL_COLUMNS = (V, 384, 0, 0)


def entries(lists, start, count):
    return lists[:, start // LANES : (start + count) // LANES]


def tile_picked_keysq_none_p_kernel(tc, x_words, x_scales, w1, w2, ga, gb, offs, two, n1, nq, cq, out):
    nc = tc.nc
    with ExitStack() as ctx:
        lists = ctx.enter_context(tc.tile_pool(name="lists", bufs=1))
        keep = ctx.enter_context(tc.tile_pool(name="keep", bufs=1))
        psum = ctx.enter_context(tc.psum_pool(name="psum", bufs=1))

        def sb(name, shape, dtype):
            return keep.tile(shape, dtype, name=name, tag=name, align_bytes=64)

        def bank(number, width):
            return psum.tile([P, width], F32, name="bank%d" % number, tag="bank%d" % number)

        offs_sb = lists.tile([P, S // LANES], U16, name="offs_sb")
        two_sb = lists.tile([P, V // LANES], U16, name="two_sb")
        n1_sb = lists.tile([P, S // LANES], U16, name="n1_sb")
        nq_sb = lists.tile([P, V // LANES], U16, name="nq_sb")
        cq_sb = lists.tile([P, V // LANES], U16, name="cq_sb")

        words = sb("words", [P, T], U32)
        scales = sb("scales", [P, T], U8)
        w1_raw = [sb("w1_raw%d" % h, [P, R, HALF], F32) for h in range(2)]
        w2_raw = sb("w2_raw", [P, R, H], F32)
        ga_sb = sb("ga_sb", [P, R], F32)
        gb_sb = sb("gb_sb", [P, R], F32)

        nc.sync.dma_start(two_sb[:], two)
        for q in range(4):
            rows = x_scales[0, 4 * q : 4 * q + 4, :].bitcast(I32)
            nc.sync.dma_start(scales[32 * q : 32 * q + 32, :].bitcast(I32), rows.unsqueeze(0).to_broadcast([8, 4, T // 4]))
        nc.sync.dma_start(offs_sb[:], offs)
        nc.sync.dma_start(ga_sb[:], ga.rearrange("(p t) o -> p (t o)", t=R))
        nc.sync.dma_start(words[:].bitcast(I32), x_words[0].rearrange("p n r -> p (n r)").bitcast(I32))
        nc.sync.dma_start(gb_sb[:], gb.rearrange("(p t) o -> p (t o)", t=R))
        nc.sync.dma_start(w2_raw[:], w2.rearrange("(p j) c -> p j c", j=R))
        for h in range(2):
            nc.sync.dma_start(w1_raw[h][:], w1.rearrange("(p j) c -> p j c", j=R)[:, :, HALF * h : HALF * (h + 1)])
        nc.sync.dma_start(nq_sb[:], nq)
        nc.sync.dma_start(n1_sb[:], n1)
        nc.sync.dma_start(cq_sb[:], cq)

        half = sb("half", [P, R], F32)
        nc.gpsimd.memset(half[:], 0.5)
        warm = sb("warm", [P, 1], F32)
        nc.scalar.activation(warm[:], half[:, 0:1], ACT.Tanh)

        nonneg = sb("nonneg", [P, R], F32)
        sign = sb("sign", [P, R], F32)
        size = sb("size", [P, R], F32)
        root = sb("root", [P, R], F32)
        nc.gpsimd.tensor_scalar(nonneg[:], ga_sb[:], 0.0, 2.0, ALU.is_ge, ALU.mult)
        nc.gpsimd.tensor_scalar(sign[:], nonneg[:], -1.0, 1.0, ALU.add, ALU.mult)
        nc.gpsimd.tensor_tensor(size[:], ga_sb[:], sign[:], ALU.mult)
        nc.gpsimd.tensor_tensor(root[:], size[:], half[:], ALU.pow)

        gb_wide = sb("gb_wide", [P, R, EARLY], F32)
        nc.scalar.copy(gb_wide[:], gb_sb[:].unsqueeze(2).to_broadcast([P, R, EARLY]))

        two_scales = sb("two_scales", [P, V], U8)
        offs_scales = sb("offs_scales", [P, S], U8)
        two_words = sb("two_words", [P, V], U32)
        offs_words = sb("offs_words", [P, S], U32)
        nc.vector.tensor_copy(two_scales[:], scales[:].indirect(two_sb[:]))
        nc.vector.tensor_copy(offs_scales[:], scales[:].indirect(offs_sb[:]))
        nc.vector.tensor_copy(two_words[:], words[:].indirect(two_sb[:]))
        nc.vector.tensor_copy(offs_words[:], words[:].indirect(offs_sb[:]))

        def quantize(name, values, width):
            codes = sb(name + "_codes", [P, width], U32)
            plane = sb(name + "_plane", [P, width], U8)
            nc.vector.quantize_mx(out=codes[:].bitcast(FP8X4), scales=plane[:], in_=values)
            return codes, plane

        def round_weights(rounded, raw, pair, copy):
            copy(rounded.rearrange("p t m j -> p m j t"), raw.rearrange("p j (m t) -> p m j t", t=R)[:, :, :, 2 * pair : 2 * pair + 2])

        def quantize_pair(name, rounded):
            return quantize(name, rounded[:].rearrange("p t m j -> p (t m j)"), 2 * P)

        def product(acc, left, column, right, start, count):
            nc.tensor.matmul_mx(
                out=acc,
                lhsT=left[0][:, column : column + P].bitcast(FP8X4),
                lhsT_scale=left[1][:, column : column + P],
                rhs=right[0][:, start : start + count].bitcast(FP8X4),
                rhs_scale=right[1][:, start : start + count],
                start=True,
                stop=True,
            )

        w2_bf = [sb("w2_bf%d" % pair, [P, 2, P, R], BF16) for pair in range(2)]
        round_weights(w2_bf[0][:], w2_raw[:], 0, nc.vector.tensor_copy)
        round_weights(w2_bf[1][:], w2_raw[:], 1, nc.scalar.copy)
        w2_q = [quantize_pair("w2_%d" % pair, w2_bf[pair]) for pair in range(2)]
        tanh_b = [sb("tanh_b%d" % t, [P, V], F32) for t in range(R)]


        def make_tanh(number, t, start, count):
            acc = bank(number, count)
            product(acc[:], w2_q[t // 2], P * (t % 2), (two_words, two_scales), start, count)
            nc.scalar.activation(tanh_b[t][:, start : start + count], acc[:], ACT.Tanh, scale=sign[:, t : t + 1])

        def gather_early(t):
            nc.vector.tensor_tensor(early[:, t, :], tanh_b[t][:].indirect(entries(nq_sb, 0, EARLY)), gb_wide[:, t, :], ALU.mult)

        make_tanh(0, 0, 0, HALF)
        make_tanh(1, 0, HALF, HALF)
        for t in range(1, R):
            make_tanh(t + 1, t, 0, V)
        w1_bf = [sb("w1_bf%d" % pair, [P, 2, P, R], BF16) for pair in range(2)]
        round_weights(w1_bf[0][:, :, 0:64], w1_raw[0][:], 0, nc.vector.tensor_copy)
        round_weights(w1_bf[1][:, :, 0:64], w1_raw[0][:], 1, nc.vector.tensor_copy)
        round_weights(w1_bf[0][:, :, 64:P], w1_raw[1][:], 0, nc.vector.tensor_copy)
        round_weights(w1_bf[1][:, :, 64:P], w1_raw[1][:], 1, nc.scalar.copy)
        w1_q = [quantize_pair("w1_%d" % pair, w1_bf[pair]) for pair in range(2)]
        early = keep.tile([P, R, EARLY], F32, name="z2_early", tag="w1_bf0", align_bytes=64)
        for t in range(R):
            gather_early(t)

        s_tiles = [sb("s_tile%d" % u, [P, 2 * V], F32) for u in range(R)]
        diff = [sb("diff%d" % h, [P, R, HALF], F32) for h in range(2)]

        def make_diff(t):
            acc = bank((5 + t) % 8, S)
            product(acc[:], w1_q[t // 2], P * (t % 2), (offs_words, offs_scales), 0, S)
            window = sb("a_window%d" % t, [P, S], F32)
            plain = s_tiles[t][:, V : 2 * V]
            nc.scalar.activation(window[:], acc[:], ACT.Copy, scale=root[:, t : t + 1])
            nc.scalar.activation(plain, acc[:], ACT.Copy, scale=root[:, t : t + 1])
            for h in range(2):
                nc.vector.tensor_tensor(
                    diff[h][:, t, :], window[:].indirect(entries(n1_sb, HALF * h, HALF)), plain[:, HALF * h : HALF * (h + 1)], ALU.subtract
                )

        for t in range(R):
            make_diff(t)
        early_bf = keep.tile([P, EARLY, R], BF16, name="z2_early_bf", tag="w1_1_codes", align_bytes=64)
        nc.scalar.copy(early_bf[:].rearrange("p (c i) t -> p c t i", i=4), early[:].rearrange("p t (c i) -> p c t i", i=4))
        z_bf = sb("z_bf", [P, R, P, R], BF16)
        for h in range(2):
            nc.scalar.activation(
                z_bf[:].rearrange("p u m t -> p m t u")[:, 64 * h : 64 * (h + 1)],
                diff[h][:].rearrange("p t (m u) -> p m t u", u=R),
                ACT.Square,
            )

        late = keep.tile([P, R, LATE], F32, name="z2_late", tag="a_window3", align_bytes=64)
        for t in range(R):
            nc.vector.tensor_tensor(late[:, t, :], tanh_b[t][:].indirect(entries(nq_sb, EARLY, LATE)), gb_wide[:, t, 0:LATE], ALU.mult)
        z2_codes = sb("z2_codes", [P, V], U32)
        z2_plane = sb("z2_plane", [P, V], U8)

        def quantize_z2(start, count, values):
            nc.vector.quantize_mx(
                out=z2_codes[:, start : start + count].bitcast(FP8X4),
                scales=z2_plane[:, start : start + count],
                in_=values.rearrange("p v t -> p (v t)"),
            )

        def quantize_z(u):
            return quantize("z_%d" % u, z_bf[:, u].rearrange("p m t -> p (m t)"), P)

        quantize_z2(0, HALF, early_bf[:, 0:HALF])
        quantize_z2(HALF, EARLY - HALF, early_bf[:, HALF:EARLY])
        z_q = [quantize_z(0)]
        late_bf = z_bf[:, 0]
        nc.vector.tensor_copy(late_bf.rearrange("p (c i) t -> p c t i", i=4), late[:].rearrange("p t (c i) -> p c t i", i=4))
        quantize_z2(EARLY, LATE, late_bf)
        z_q.extend(quantize_z(u) for u in range(1, R))

        next_bank = 0
        out_rows = out.rearrange("(p u) v -> p u v", u=R)
        for u in range(R):
            window = s_tiles[u]
            pieces = ((0, HALF), (HALF, EARLY - HALF), (EARLY, LATE)) if u == 0 else ((0, V),)
            for start, count in pieces:
                acc = bank(next_bank, count)
                next_bank += 1
                product(acc[:], z_q[u], 0, (z2_codes, z2_plane), start, count)
                nc.scalar.activation(window[:, start : start + count], acc[:], ACT.Copy, scale=0.0625)
            fetched = sb("s_fetched%d" % u, [P, V], F32)
            larger = sb("s_larger%d" % u, [P, V], F32)
            split = POOL_COLUMNS[u]
            if split:
                excess = sb("s_excess%d" % u, [P, split], F32)
                gain = sb("s_gain%d" % u, [P, split], F32)
                nc.vector.tensor_copy(fetched[:], window[:].indirect(cq_sb[:]))
                nc.gpsimd.tensor_tensor(excess[:], fetched[:, 0:split], window[:, 0:split], ALU.subtract)
                nc.scalar.activation(gain[:], excess[:], ACT.Relu)
                nc.gpsimd.tensor_tensor(larger[:, 0:split], gain[:], window[:, 0:split], ALU.add)
                nc.scalar.dma_start(out_rows[:, u, 0:split], larger[:, 0:split])
                rest = [slice(split, V)] if split < V else []
            else:
                rest = [slice(0, HALF), slice(HALF, V)]
                for columns in rest:
                    nc.vector.tensor_copy(fetched[:, columns], window[:].indirect(entries(cq_sb, columns.start, HALF)))
            for columns in rest:
                nc.vector.scalar_tensor_tensor(larger[:, columns], acc[:, columns], 0.0625, fetched[:, columns], ALU.mult, ALU.max)
                nc.sync.dma_start(out_rows[:, u, columns], larger[:, columns])
